import numpy as np
import ml_dtypes


def mxq(x, axis, fmt="e4m3"):
    dtype, down = {"e4m3": (ml_dtypes.float8_e4m3fn, 7), "e5m2": (ml_dtypes.float8_e5m2, 14)}[fmt]
    v = np.moveaxis(np.asarray(x, np.float32).astype(ml_dtypes.bfloat16).astype(np.float64), axis, -1)
    blocks = v.reshape(v.shape[:-1] + (-1, 32))
    amax = np.abs(blocks).max(-1, keepdims=True)
    byte = np.maximum(np.where(amax > 0, np.frexp(amax)[1] - 1 + 127, 0) - down, 1)
    scale = np.exp2(byte - 127.0)
    codes = (blocks / scale).astype(np.float32).astype(dtype).astype(np.float64)
    return np.moveaxis((codes * scale).reshape(v.shape), -1, axis)


WIDE = False


def mx_kscale(k):
    if not WIDE:
        return np.ones(k)
    levels = np.array([10, -10, 5, -5, 0])
    if k % 512:
        return np.exp2(np.random.permutation(np.resize(levels, k // 32))).repeat(32)
    a = np.empty((k // 512, 16))
    for p in range(k // 512):
        a[p, :8] = np.random.permutation(np.resize(levels, 8))
        for g in range(8):
            far = levels[np.abs(levels - a[p, g]) >= 10]
            a[p, g + 8] = far[np.random.randint(len(far))]
    return np.exp2(a.ravel()).repeat(32)


def f64(x):
    return np.asarray(x).astype(np.float64)


def striped(idx):
    return np.tile(idx.reshape(-1, 16).T, (8, 1)).astype(np.uint16)


def unstriped(offs):
    return offs[:16].T.reshape(-1).astype(np.int64)


K, T, E, C, N = 512, 2048, 2, 256, 128


def by_expert(wq, xq):
    return np.concatenate([wq[e].T @ xq[:, e * C:(e + 1) * C] for e in range(E)], axis=1)


def setup_inputs():
    n = np.random.standard_normal
    s = mx_kscale(K)[:, None]
    return {
        "xT": (n((K, T)) * s).astype(np.float32),
        "w": (n((E, K, N)) / np.sqrt(K) / s[None]).astype(np.float32),
        "gate": np.tile(np.random.uniform(0.2, 1.0, E * C), (N, 1)).astype(np.float32),
        "offs": striped(np.random.permutation(T)[:E * C]),
    }


def reference(xT, w, gate, offs):
    idx = unstriped(offs)
    xq = mxq(f64(xT)[:, idx], 0, "e4m3")
    y = by_expert(mxq(f64(w), 1, "e4m3"), xq)
    out = np.zeros((N, T))
    out[:, idx] = f64(gate) * y
    return out

@@ -1,0 +1,93 @@
+from contextlib import ExitStack
+
+import concourse.mybir as mybir
+
+K, T, E, C, N = 512, 2048, 2, 256, 128
+FLOPS = 2 * K * E * C * N
+
+F32 = mybir.dt.float32
+BF16 = mybir.dt.bfloat16
+U32 = mybir.dt.uint32
+U16 = mybir.dt.uint16
+U8 = mybir.dt.uint8
+FP8X4 = mybir.dt.float8_e4m3fn_x4
+MULT = mybir.AluOpType.mult
+
+P = 128
+PACK = 4
+COLS = C // 16
+
+
+def tile_routed_moe_kernel(tc, xT, w, gate, offs, out):
+    nc = tc.nc
+    with ExitStack() as ctx:
+        keep = ctx.enter_context(tc.tile_pool(name="keep", bufs=1))
+        psum = ctx.enter_context(tc.psum_pool(name="psum", bufs=1))
+
+        offsets = keep.tile([P, E * COLS], U16, name="offsets")
+        nc.sync.dma_start(offsets[:], offs)
+
+        w_raw = keep.tile([P, E, PACK, N], F32, name="w_raw")
+        nc.sync.dma_start(out=w_raw[:], in_=w.rearrange("e (p j) n -> p e j n", j=PACK))
+
+        x_planes = xT.rearrange("(p t) n -> p t n", t=PACK)
+        planes = []
+        for t in range(PACK):
+            plane = keep.tile([P, T], F32, name="plane%d" % t)
+            nc.sync.dma_start(out=plane[:], in_=x_planes[:, t, :])
+            planes.append(plane)
+
+        gate_sb = keep.tile([P, E * C], F32, name="gate_sb")
+        nc.sync.dma_start(out=gate_sb[:], in_=gate)
+
+        window = keep.tile([P, T], F32, name="window")
+        nc.vector.memset(window[:], 0.0)
+
+        w_grp = keep.tile([P, E, N, PACK], BF16, name="w_grp", align_bytes=64)
+        nc.scalar.copy(out=w_grp[:], in_=w_raw[:].rearrange("p e j n -> p e n j"))
+        w_codes = keep.tile([P, E * N], U32, name="w_codes", align_bytes=64)
+        w_scales = keep.tile([P, E * N], U8, name="w_scales", align_bytes=64)
+        nc.vector.quantize_mx(
+            out=w_codes[:].bitcast(FP8X4),
+            scales=w_scales[:],
+            in_=w_grp[:].rearrange("p e n j -> p (e n j)"),
+        )
+
+        x_grp = [keep.tile([P, C, PACK], BF16, name="x_grp%d" % e, align_bytes=64) for e in range(E)]
+        x_codes = [keep.tile([P, C], U32, name="x_codes%d" % e, align_bytes=64) for e in range(E)]
+        x_scales = [keep.tile([P, C], U8, name="x_scales%d" % e, align_bytes=64) for e in range(E)]
+        acc = [psum.tile([N, C], F32, name="acc%d" % e) for e in range(E)]
+        y = [keep.tile([N, C], F32, name="y%d" % e) for e in range(E)]
+
+        for t in range(PACK - 1):
+            for e in range(E):
+                nc.vector.tensor_copy(
+                    out=x_grp[e][:, :, t],
+                    in_=planes[t][:].indirect(offsets[:, e * COLS : (e + 1) * COLS]),
+                )
+        for e in range(E):
+            nc.vector.tensor_copy(
+                out=x_grp[e][:, :, PACK - 1],
+                in_=planes[PACK - 1][:].indirect(offsets[:, e * COLS : (e + 1) * COLS]),
+            )
+            nc.vector.quantize_mx(
+                out=x_codes[e][:].bitcast(FP8X4),
+                scales=x_scales[e][:],
+                in_=x_grp[e][:].rearrange("p c j -> p (c j)"),
+            )
+            nc.tensor.matmul_mx(
+                out=acc[e][:],
+                lhsT=w_codes[:, e * N : (e + 1) * N].bitcast(FP8X4),
+                lhsT_scale=w_scales[:, e * N : (e + 1) * N],
+                rhs=x_codes[e][:].bitcast(FP8X4),
+                rhs_scale=x_scales[e][:],
+                start=True,
+                stop=True,
+            )
+        for e in range(E):
+            nc.vector.tensor_tensor(out=y[e][:], in0=acc[e][:], in1=gate_sb[:, e * C : (e + 1) * C], op=MULT)
+            nc.vector.tensor_copy(
+                out=window[:].indirect(offsets[:, e * COLS : (e + 1) * COLS]),
+                in_=y[e][:],
+            )
+        nc.sync.dma_start(out=out, in_=window[:])

@@ -27,9 +27,6 @@ def tile_routed_moe_kernel(tc, xT, w, gate, offs, out):
         offsets = keep.tile([P, E * COLS], U16, name="offsets")
         nc.sync.dma_start(offsets[:], offs)
 
-        w_raw = keep.tile([P, E, PACK, N], F32, name="w_raw")
-        nc.sync.dma_start(out=w_raw[:], in_=w.rearrange("e (p j) n -> p e j n", j=PACK))
-
         x_planes = xT.rearrange("(p t) n -> p t n", t=PACK)
         planes = []
         for t in range(PACK):
@@ -37,21 +34,19 @@ def tile_routed_moe_kernel(tc, xT, w, gate, offs, out):
             nc.sync.dma_start(out=plane[:], in_=x_planes[:, t, :])
             planes.append(plane)
 
+        w_raw = [keep.tile([P, PACK, N], F32, name="w_raw%d" % e) for e in range(E)]
+        for e in range(E):
+            nc.sync.dma_start(out=w_raw[e][:], in_=w[e].rearrange("(p j) n -> p j n", j=PACK))
+
         gate_sb = keep.tile([P, E * C], F32, name="gate_sb")
         nc.sync.dma_start(out=gate_sb[:], in_=gate)
 
         window = keep.tile([P, T], F32, name="window")
         nc.vector.memset(window[:], 0.0)
 
-        w_grp = keep.tile([P, E, N, PACK], BF16, name="w_grp", align_bytes=64)
-        nc.scalar.copy(out=w_grp[:], in_=w_raw[:].rearrange("p e j n -> p e n j"))
-        w_codes = keep.tile([P, E * N], U32, name="w_codes", align_bytes=64)
-        w_scales = keep.tile([P, E * N], U8, name="w_scales", align_bytes=64)
-        nc.vector.quantize_mx(
-            out=w_codes[:].bitcast(FP8X4),
-            scales=w_scales[:],
-            in_=w_grp[:].rearrange("p e n j -> p (e n j)"),
-        )
+        w_grp = [keep.tile([P, N, PACK], BF16, name="w_grp%d" % e, align_bytes=64) for e in range(E)]
+        w_codes = [keep.tile([P, N], U32, name="w_codes%d" % e, align_bytes=64) for e in range(E)]
+        w_scales = [keep.tile([P, N], U8, name="w_scales%d" % e, align_bytes=64) for e in range(E)]
 
         x_grp = [keep.tile([P, C, PACK], BF16, name="x_grp%d" % e, align_bytes=64) for e in range(E)]
         x_codes = [keep.tile([P, C], U32, name="x_codes%d" % e, align_bytes=64) for e in range(E)]
@@ -75,10 +70,16 @@ def tile_routed_moe_kernel(tc, xT, w, gate, offs, out):
                 scales=x_scales[e][:],
                 in_=x_grp[e][:].rearrange("p c j -> p (c j)"),
             )
+            nc.scalar.copy(out=w_grp[e][:], in_=w_raw[e][:].rearrange("p j n -> p n j"))
+            nc.vector.quantize_mx(
+                out=w_codes[e][:].bitcast(FP8X4),
+                scales=w_scales[e][:],
+                in_=w_grp[e][:].rearrange("p n j -> p (n j)"),
+            )
             nc.tensor.matmul_mx(
                 out=acc[e][:],
-                lhsT=w_codes[:, e * N : (e + 1) * N].bitcast(FP8X4),
-                lhsT_scale=w_scales[:, e * N : (e + 1) * N],
+                lhsT=w_codes[e][:].bitcast(FP8X4),
+                lhsT_scale=w_scales[e][:],
                 rhs=x_codes[e][:].bitcast(FP8X4),
                 rhs_scale=x_scales[e][:],
                 start=True,

@@ -30,18 +30,18 @@ def tile_routed_moe_kernel(tc, xT, w, gate, offs, out):
         x_planes = xT.rearrange("(p t) n -> p t n", t=PACK)
         planes = []
         for t in range(PACK):
-            plane = keep.tile([P, T], F32, name="plane%d" % t)
+            plane = keep.tile([P, T], F32, name="plane%d" % t, align_bytes=256)
             nc.sync.dma_start(out=plane[:], in_=x_planes[:, t, :])
             planes.append(plane)
 
-        w_raw = [keep.tile([P, PACK, N], F32, name="w_raw%d" % e) for e in range(E)]
+        w_raw = [keep.tile([P, PACK, N], F32, name="w_raw%d" % e, align_bytes=256) for e in range(E)]
         for e in range(E):
             nc.sync.dma_start(out=w_raw[e][:], in_=w[e].rearrange("(p j) n -> p j n", j=PACK))
 
-        gate_sb = keep.tile([P, E * C], F32, name="gate_sb")
+        gate_sb = keep.tile([P, E * C], F32, name="gate_sb", align_bytes=256)
         nc.sync.dma_start(out=gate_sb[:], in_=gate)
 
-        window = keep.tile([P, T], F32, name="window")
+        window = keep.tile([P, T], F32, name="window", align_bytes=256)
         nc.vector.memset(window[:], 0.0)
 
         w_grp = [keep.tile([P, N, PACK], BF16, name="w_grp%d" % e, align_bytes=64) for e in range(E)]

@@ -25,7 +25,6 @@ def tile_routed_moe_kernel(tc, xT, w, gate, offs, out):
         psum = ctx.enter_context(tc.psum_pool(name="psum", bufs=1))
 
         offsets = keep.tile([P, E * COLS], U16, name="offsets")
-        nc.sync.dma_start(offsets[:], offs)
 
         x_planes = xT.rearrange("(p t) n -> p t n", t=PACK)
         planes = []
@@ -33,6 +32,8 @@ def tile_routed_moe_kernel(tc, xT, w, gate, offs, out):
             plane = keep.tile([P, T], F32, name="plane%d" % t, align_bytes=256)
             nc.sync.dma_start(out=plane[:], in_=x_planes[:, t, :])
             planes.append(plane)
+            if t == 0:
+                nc.sync.dma_start(offsets[:], offs)
 
         w_raw = [keep.tile([P, PACK, N], F32, name="w_raw%d" % e, align_bytes=256) for e in range(E)]
         for e in range(E):

@@ -88,6 +88,7 @@ def tile_routed_moe_kernel(tc, xT, w, gate, offs, out):
             )
         for e in range(E):
             nc.vector.tensor_tensor(out=y[e][:], in0=acc[e][:], in1=gate_sb[:, e * C : (e + 1) * C], op=MULT)
+        for e in range(E):
             nc.vector.tensor_copy(
                 out=window[:].indirect(offsets[:, e * COLS : (e + 1) * COLS]),
                 in_=y[e][:],

from contextlib import ExitStack

import concourse.mybir as mybir

K, T, E, C, N = 512, 2048, 2, 256, 128
FLOPS = 2 * K * E * C * N

F32 = mybir.dt.float32
BF16 = mybir.dt.bfloat16
U32 = mybir.dt.uint32
U16 = mybir.dt.uint16
U8 = mybir.dt.uint8
FP8X4 = mybir.dt.float8_e4m3fn_x4
MULT = mybir.AluOpType.mult

P = 128
PACK = 4
COLS = C // 16


def tile_routed_moe_kernel(tc, xT, w, gate, offs, out):
    nc = tc.nc
    with ExitStack() as ctx:
        keep = ctx.enter_context(tc.tile_pool(name="keep", bufs=1))
        psum = ctx.enter_context(tc.psum_pool(name="psum", bufs=1))

        offsets = keep.tile([P, E * COLS], U16, name="offsets")

        x_planes = xT.rearrange("(p t) n -> p t n", t=PACK)
        planes = []
        for t in range(PACK):
            plane = keep.tile([P, T], F32, name="plane%d" % t, align_bytes=256)
            nc.sync.dma_start(out=plane[:], in_=x_planes[:, t, :])
            planes.append(plane)
            if t == 0:
                nc.sync.dma_start(offsets[:], offs)

        w_raw = [keep.tile([P, PACK, N], F32, name="w_raw%d" % e, align_bytes=256) for e in range(E)]
        for e in range(E):
            nc.sync.dma_start(out=w_raw[e][:], in_=w[e].rearrange("(p j) n -> p j n", j=PACK))

        gate_sb = keep.tile([P, E * C], F32, name="gate_sb", align_bytes=256)
        nc.sync.dma_start(out=gate_sb[:], in_=gate)

        window = keep.tile([P, T], F32, name="window", align_bytes=256)
        nc.vector.memset(window[:], 0.0)

        w_grp = [keep.tile([P, N, PACK], BF16, name="w_grp%d" % e, align_bytes=64) for e in range(E)]
        w_codes = [keep.tile([P, N], U32, name="w_codes%d" % e, align_bytes=64) for e in range(E)]
        w_scales = [keep.tile([P, N], U8, name="w_scales%d" % e, align_bytes=64) for e in range(E)]

        x_grp = [keep.tile([P, C, PACK], BF16, name="x_grp%d" % e, align_bytes=64) for e in range(E)]
        x_codes = [keep.tile([P, C], U32, name="x_codes%d" % e, align_bytes=64) for e in range(E)]
        x_scales = [keep.tile([P, C], U8, name="x_scales%d" % e, align_bytes=64) for e in range(E)]
        acc = [psum.tile([N, C], F32, name="acc%d" % e) for e in range(E)]
        y = [keep.tile([N, C], F32, name="y%d" % e) for e in range(E)]

        for t in range(PACK - 1):
            for e in range(E):
                nc.vector.tensor_copy(
                    out=x_grp[e][:, :, t],
                    in_=planes[t][:].indirect(offsets[:, e * COLS : (e + 1) * COLS]),
                )
        for e in range(E):
            nc.vector.tensor_copy(
                out=x_grp[e][:, :, PACK - 1],
                in_=planes[PACK - 1][:].indirect(offsets[:, e * COLS : (e + 1) * COLS]),
            )
            nc.vector.quantize_mx(
                out=x_codes[e][:].bitcast(FP8X4),
                scales=x_scales[e][:],
                in_=x_grp[e][:].rearrange("p c j -> p (c j)"),
            )
            nc.scalar.copy(out=w_grp[e][:], in_=w_raw[e][:].rearrange("p j n -> p n j"))
            nc.vector.quantize_mx(
                out=w_codes[e][:].bitcast(FP8X4),
                scales=w_scales[e][:],
                in_=w_grp[e][:].rearrange("p n j -> p (n j)"),
            )
            nc.tensor.matmul_mx(
                out=acc[e][:],
                lhsT=w_codes[e][:].bitcast(FP8X4),
                lhsT_scale=w_scales[e][:],
                rhs=x_codes[e][:].bitcast(FP8X4),
                rhs_scale=x_scales[e][:],
                start=True,
                stop=True,
            )
        for e in range(E):
            nc.vector.tensor_tensor(out=y[e][:], in0=acc[e][:], in1=gate_sb[:, e * C : (e + 1) * C], op=MULT)
        for e in range(E):
            nc.vector.tensor_copy(
                out=window[:].indirect(offsets[:, e * COLS : (e + 1) * COLS]),
                in_=y[e][:],
            )
        nc.sync.dma_start(out=out, in_=window[:])
